import numpy as np
import ml_dtypes


def mxq(x, axis, fmt="e4m3"):
    dtype, down = {"e4m3": (ml_dtypes.float8_e4m3fn, 7), "e5m2": (ml_dtypes.float8_e5m2, 14)}[fmt]
    v = np.moveaxis(np.asarray(x, np.float32).astype(ml_dtypes.bfloat16).astype(np.float64), axis, -1)
    blocks = v.reshape(v.shape[:-1] + (-1, 32))
    amax = np.abs(blocks).max(-1, keepdims=True)
    byte = np.maximum(np.where(amax > 0, np.frexp(amax)[1] - 1 + 127, 0) - down, 1)
    scale = np.exp2(byte - 127.0)
    codes = (blocks / scale).astype(np.float32).astype(dtype).astype(np.float64)
    return np.moveaxis((codes * scale).reshape(v.shape), -1, axis)


WIDE = False


def mx_kscale(k):
    if not WIDE:
        return np.ones(k)
    levels = np.array([30, -30])
    if k % 512:
        return np.exp2(np.random.permutation(np.resize(levels, k // 32))).repeat(32)
    a = np.empty((k // 512, 16))
    for p in range(k // 512):
        a[p, :8] = np.random.permutation(np.resize(levels, 8))
        for g in range(8):
            far = levels[np.abs(levels - a[p, g]) >= 10]
            a[p, g + 8] = far[np.random.randint(len(far))]
    return np.exp2(a.ravel()).repeat(32)


BF16 = ml_dtypes.bfloat16


def bf(x):
    return np.asarray(x, np.float32).astype(BF16)


def f64(x):
    return np.asarray(x).astype(np.float64)


E2M1 = np.array([0.0, 0.5, 1.0, 1.5, 2.0, 3.0, 4.0, 6.0, -0.0, -0.5, -1.0, -1.5, -2.0, -3.0, -4.0, -6.0])


def pack_weight(w, fmt):
    k, n = w.shape
    w = f64(bf(w)).reshape(k // 32, 32, n)
    amax = np.abs(w).max(1)
    if fmt in ("e4m3", "e5m2"):
        byte = np.frexp(amax)[1] - 1 + 127 - (7 if fmt == "e4m3" else 14)
    else:
        mant, ex = np.frexp(amax / 6.0)
        byte = np.where(mant > 0.5, ex, ex - 1) + 127
    byte = np.clip(np.where(amax > 0, byte, 1), 1, 254)
    scaled = (w * np.exp2(127.0 - byte)[:, None, :]).reshape(k, n).astype(np.float32)
    by_word = np.ascontiguousarray(scaled.reshape(k // 512, 128, 4, n).transpose(0, 1, 3, 2))
    if fmt in ("e4m3", "e5m2"):
        words = by_word.astype(ml_dtypes.float8_e4m3fn if fmt == "e4m3" else ml_dtypes.float8_e5m2).view(np.uint8)
    else:
        c = by_word.astype(ml_dtypes.float4_e2m1fn).view(np.uint8) & 0xF
        words = c[..., 0::2] | (c[..., 1::2] << 4)
    return np.ascontiguousarray(words), np.ascontiguousarray(byte.astype(np.uint8).reshape(k // 512, 16, n))


def unpack_weight(words, scales, fmt):
    g, p, n, _ = words.shape
    if fmt in ("e4m3", "e5m2"):
        vals = np.ascontiguousarray(words).view(ml_dtypes.float8_e4m3fn if fmt == "e4m3" else ml_dtypes.float8_e5m2).astype(np.float64)
    else:
        nib = np.empty((g, p, n, 4), np.uint8)
        nib[..., 0::2] = words & 0xF
        nib[..., 1::2] = words >> 4
        vals = E2M1[nib]
    vals = vals * np.repeat(np.exp2(scales.astype(np.float64) - 127.0), 8, axis=1)[..., None]
    return vals.transpose(0, 1, 3, 2).reshape(g * 512, n)


K, T, L, C, B = 4096, 128, 8, 512, 32


def setup_inputs():
    s = mx_kscale(K)
    leaf = (np.argsort(np.random.random_sample((K // B, B, T)), axis=1) % L).reshape(K, T)
    boot = np.random.exponential(1.0, (K, T))
    member = (boot[:, :, None] * (leaf[:, :, None] == np.arange(L))).reshape(K, T * L)
    e = np.exp(np.random.standard_normal((K, C)))
    labels = np.random.randint(0, C, K)
    G = e / e.sum(axis=1, keepdims=True) - (labels[:, None] == np.arange(C))
    G_words, G_scales = pack_weight(G / s[:, None], "e5m2")
    return {"member": bf(member * s[:, None]),
            "grad_words": G_words,
            "grad_scales": G_scales,
            "curv": bf(0.5 + np.random.random_sample((T * L, C))),
            "old": bf(np.random.standard_normal((T * L, C)))}


def reference(member, grad_words, grad_scales, curv, old):
    G = unpack_weight(grad_words, grad_scales, "e5m2")
    A = mxq(f64(member), 0, "e4m3")
    S = A.T @ G
    h = f64(curv)
    return (h * f64(old) - S) / (h + 1.0)

@@ -1,0 +1,194 @@
+from contextlib import ExitStack
+
+import concourse.mybir as mybir
+
+K, LEAVES, CLASSES = 4096, 1024, 512
+FLOPS = 2 * K * LEAVES * CLASSES
+
+F32 = mybir.dt.float32
+BF16 = mybir.dt.bfloat16
+U32 = mybir.dt.uint32
+I32 = mybir.dt.int32
+U8 = mybir.dt.uint8
+E4M3 = mybir.dt.float8_e4m3fn_x4
+E5M2 = mybir.dt.float8_e5m2_x4
+ADD = mybir.AluOpType.add
+SUB = mybir.AluOpType.subtract
+MUL = mybir.AluOpType.mult
+RSQRT = mybir.ActivationFunctionType.Abs_reciprocal_sqrt
+SQUARE = mybir.ActivationFunctionType.Square
+
+P = 128
+PACK = 4
+GROUPS = K // (P * PACK)
+HALF = 512
+TILES = LEAVES // P
+CUT = 272
+LAST_CUT = 256
+
+
+def tile_boosted_leaf_refresh_e1_kernel(tc, member, grad_words, grad_scales, curv, old, out):
+    nc = tc.nc
+    with ExitStack() as ctx:
+        keep = ctx.enter_context(tc.tile_pool(name="keep", bufs=1))
+        inter = ctx.enter_context(tc.tile_pool(name="inter", bufs=4))
+        psum = ctx.enter_context(tc.psum_pool(name="psum", bufs=1))
+        ctx.enter_context(tc.manual_schedule())
+
+        a_view = member.rearrange("(g p j) w -> g p j w", p=P, j=PACK)
+        raw = {}
+        words = {}
+
+        one = keep.tile([P, 1], F32, name="one")
+        nc.vector.memset(one[:], 1.0)
+        g_scales = keep.tile([P, GROUPS, CLASSES], U8, align_bytes=64, name="g_scales")
+        nc.vector.memset(g_scales[:].rearrange("p g n -> p (g n)").bitcast(I32), 0)
+
+        def load_cols(g, lo, width):
+            t = keep.tile([P, PACK, width], BF16, align_bytes=64, name="raw_%d_%d" % (g, lo))
+            nc.sync.dma_start(out=t[:], in_=a_view[g, :, :, lo:lo + width])
+            step = min(width, HALF)
+            for c in range(0, width, step):
+                raw[(g, lo + c)] = t[:, :, c:c + step]
+
+        def load_words(g):
+            t = keep.tile([P, CLASSES], U32, align_bytes=64, name="words_%d" % g)
+            nc.sync.dma_start(out=t[:].bitcast(I32), in_=grad_words[g].rearrange("p n t -> p (n t)").bitcast(I32))
+            words[g] = t
+
+        curv_t = {}
+        old_t = {}
+
+        def load_old_curv(h):
+            for src, dst, nm in ((curv, curv_t, "curv"), (old, old_t, "old")):
+                t = keep.tile([P, TILES // 2, CLASSES], BF16, align_bytes=64, name="%s_%d" % (nm, h))
+                nc.sync.dma_start(out=t[:], in_=src[h * HALF:(h + 1) * HALF, :].rearrange("(m p) n -> p m n", p=P))
+                for m in range(TILES // 2):
+                    dst[h * TILES // 2 + m] = t[:, m, :]
+
+        def load_scales():
+            for q in range(4):
+                nc.sync.dma_start(
+                    out=g_scales[32 * q:32 * q + 4, :, :].bitcast(I32),
+                    in_=grad_scales[:, 4 * q:4 * q + 4, :].rearrange("g r n -> r g n").bitcast(I32),
+                )
+
+        load_cols(0, 0, 256)
+        load_cols(0, 256, 256)
+        load_cols(0, 512, 512)
+        load_cols(1, 0, LEAVES)
+        load_scales()
+        load_words(0)
+        load_cols(2, 0, LEAVES)
+        load_words(1)
+        load_cols(3, 0, LEAVES)
+        load_old_curv(0)
+        for g in range(4, GROUPS):
+            load_cols(g, 0, LEAVES)
+            load_words(g - 2)
+        load_words(6)
+        load_words(7)
+        load_old_curv(1)
+
+        steps = [(0, 0, 256), (0, 256, 256), (0, 512, 512)]
+        steps += [(g, h * HALF, HALF) for g in range(1, GROUPS) for h in range(2)]
+        last = len(steps) - 1
+
+        banks = []
+        for m in range(TILES):
+            bank = psum.tile([P, CLASSES], F32, name="bank_%d" % m)
+            banks.append(bank)
+        grouped = {}
+        codes = {}
+        scales = {}
+
+        def cut(i):
+            return LAST_CUT if i == last else CUT * steps[i][2] // HALF
+
+        def interleave(copy, i, lo, hi):
+            g, c0, width = steps[i]
+            copy(
+                out=grouped[i][:, lo:hi, :].rearrange("p (c i) t -> p c t i", i=4),
+                in_=raw[(g, c0)][:, :, lo:hi].rearrange("p t (c i) -> p c t i", i=4),
+            )
+
+        def copy_scalar(i):
+            t = inter.tile([P, steps[i][2], PACK], BF16, align_bytes=64, name="grouped")
+            grouped[i] = t
+            interleave(nc.scalar.copy, i, 0, cut(i))
+
+        def copy_vector(i):
+            interleave(nc.vector.tensor_copy, i, cut(i), steps[i][2])
+
+        def quantise(i):
+            width = steps[i][2]
+            c = keep.tile([P, width], U32, align_bytes=64, name="codes_%d" % i)
+            s = keep.tile([P, width], U8, align_bytes=64, name="scales_%d" % i)
+            nc.vector.quantize_mx(out=c[:].bitcast(E4M3), scales=s[:], in_=grouped[i][:].rearrange("p w j -> p (w j)"))
+            codes[i], scales[i] = c, s
+
+        def multiply(i):
+            g, c0, width = steps[i]
+            for m in range(width // P):
+                cols = slice(m * P, (m + 1) * P)
+                nc.tensor.matmul_mx(
+                    out=banks[c0 // P + m][:],
+                    lhsT=codes[i][:, cols].bitcast(E4M3),
+                    lhsT_scale=scales[i][:, cols],
+                    rhs=words[g][:].bitcast(E5M2),
+                    rhs_scale=g_scales[:, g, :],
+                    start=(g == 0),
+                    stop=(g == GROUPS - 1),
+                )
+
+        recip = {}
+        diff = {}
+
+        def reciprocal(m):
+            r = keep.tile([P, CLASSES], F32, name="recip_%d" % m)
+            nc.scalar.activation(out=r[:], in_=curv_t[m], func=RSQRT, bias=one[:], scale=1.0)
+            nc.scalar.activation(out=r[:], in_=r[:], func=SQUARE)
+            recip[m] = r
+
+        def product(m):
+            d = keep.tile([P, CLASSES], F32, name="diff_%d" % m)
+            nc.vector.tensor_tensor(out=d[:], in0=curv_t[m], in1=old_t[m], op=MUL)
+            diff[m] = d
+
+        def subtract(m):
+            nc.vector.tensor_tensor(out=diff[m][:], in0=diff[m][:], in1=banks[m][:], op=SUB)
+
+        def finish(m):
+            o = keep.tile([P, CLASSES], F32, name="result_%d" % m)
+            nc.vector.tensor_tensor(out=o[:], in0=diff[m][:], in1=recip[m][:], op=MUL)
+            nc.sync.dma_start(out=out[m * P:(m + 1) * P, :], in_=o[:])
+
+        early = 8
+        half = TILES // 2
+        for i in range(len(steps)):
+            copy_scalar(i)
+            if early <= i < early + half:
+                reciprocal(i - early)
+            copy_vector(i)
+            if i > 0:
+                quantise(i - 1)
+                multiply(i - 1)
+            if early <= i < early + half:
+                product(i - early)
+        for m in range(half, TILES):
+            reciprocal(m)
+        quantise(last)
+        multiply(last)
+        subtract(0)
+        for m in range(1, half):
+            subtract(m)
+            finish(m - 1)
+        product(half)
+        finish(half - 1)
+        for m in range(half + 1, TILES):
+            product(m)
+        subtract(half)
+        for m in range(half + 1, TILES):
+            subtract(m)
+            finish(m - 1)
+        finish(TILES - 1)

@@ -21,10 +21,9 @@ SQUARE = mybir.ActivationFunctionType.Square
 P = 128
 PACK = 4
 GROUPS = K // (P * PACK)
-HALF = 512
 TILES = LEAVES // P
-CUT = 272
-LAST_CUT = 256
+HALF = TILES // 2
+CUT = 66
 
 
 def tile_boosted_leaf_refresh_e1_kernel(tc, member, grad_words, grad_scales, curv, old, out):
@@ -36,20 +35,22 @@ def tile_boosted_leaf_refresh_e1_kernel(tc, member, grad_words, grad_scales, cur
         ctx.enter_context(tc.manual_schedule())
 
         a_view = member.rearrange("(g p j) w -> g p j w", p=P, j=PACK)
+        out_view = out.rearrange("(p m) n -> p m n", m=TILES)
         raw = {}
         words = {}
 
         one = keep.tile([P, 1], F32, name="one")
         nc.vector.memset(one[:], 1.0)
+        warm = keep.tile([P, 1], F32, name="warm")
+        nc.scalar.activation(out=warm[:], in_=one[:], func=RSQRT, bias=one[:], scale=1.0)
         g_scales = keep.tile([P, GROUPS, CLASSES], U8, align_bytes=64, name="g_scales")
         nc.vector.memset(g_scales[:].rearrange("p g n -> p (g n)").bitcast(I32), 0)
 
-        def load_cols(g, lo, width):
-            t = keep.tile([P, PACK, width], BF16, align_bytes=64, name="raw_%d_%d" % (g, lo))
-            nc.sync.dma_start(out=t[:], in_=a_view[g, :, :, lo:lo + width])
-            step = min(width, HALF)
-            for c in range(0, width, step):
-                raw[(g, lo + c)] = t[:, :, c:c + step]
+        def load_member(g, lo, hi):
+            if g not in raw:
+                t = keep.tile([P, PACK, LEAVES], BF16, align_bytes=64, name="raw_%d" % g)
+                raw[g] = t
+            nc.sync.dma_start(out=raw[g][:, :, lo:hi], in_=a_view[g, :, :, lo:hi])
 
         def load_words(g):
             t = keep.tile([P, CLASSES], U32, align_bytes=64, name="words_%d" % g)
@@ -61,10 +62,10 @@ def tile_boosted_leaf_refresh_e1_kernel(tc, member, grad_words, grad_scales, cur
 
         def load_old_curv(h):
             for src, dst, nm in ((curv, curv_t, "curv"), (old, old_t, "old")):
-                t = keep.tile([P, TILES // 2, CLASSES], BF16, align_bytes=64, name="%s_%d" % (nm, h))
-                nc.sync.dma_start(out=t[:], in_=src[h * HALF:(h + 1) * HALF, :].rearrange("(m p) n -> p m n", p=P))
-                for m in range(TILES // 2):
-                    dst[h * TILES // 2 + m] = t[:, m, :]
+                t = keep.tile([P, HALF, CLASSES], BF16, align_bytes=64, name="%s_%d" % (nm, h))
+                nc.sync.dma_start(out=t[:], in_=src.rearrange("(p m) n -> p m n", m=TILES)[:, h * HALF:(h + 1) * HALF, :])
+                for m in range(HALF):
+                    dst[h * HALF + m] = t[:, m, :]
 
         def load_scales():
             for q in range(4):
@@ -73,25 +74,21 @@ def tile_boosted_leaf_refresh_e1_kernel(tc, member, grad_words, grad_scales, cur
                     in_=grad_scales[:, 4 * q:4 * q + 4, :].rearrange("g r n -> r g n").bitcast(I32),
                 )
 
-        load_cols(0, 0, 256)
-        load_cols(0, 256, 256)
-        load_cols(0, 512, 512)
-        load_cols(1, 0, LEAVES)
+        load_member(0, 0, TILES * CUT)
+        load_member(0, TILES * CUT, LEAVES)
+        load_member(1, 0, LEAVES)
         load_scales()
         load_words(0)
-        load_cols(2, 0, LEAVES)
-        load_words(1)
-        load_cols(3, 0, LEAVES)
-        load_old_curv(0)
-        for g in range(4, GROUPS):
-            load_cols(g, 0, LEAVES)
-            load_words(g - 2)
-        load_words(6)
-        load_words(7)
+        for g in range(2, GROUPS):
+            if g == 5:
+                load_old_curv(0)
+            if g == GROUPS - 1:
+                load_words(g - 1)
+            load_member(g, 0, LEAVES)
+            load_words(g if g == GROUPS - 1 else g - 1)
         load_old_curv(1)
 
-        steps = [(0, 0, 256), (0, 256, 256), (0, 512, 512)]
-        steps += [(g, h * HALF, HALF) for g in range(1, GROUPS) for h in range(2)]
+        steps = [(g, h) for g in range(GROUPS) for h in range(2)]
         last = len(steps) - 1
 
         banks = []
@@ -102,37 +99,33 @@ def tile_boosted_leaf_refresh_e1_kernel(tc, member, grad_words, grad_scales, cur
         codes = {}
         scales = {}
 
-        def cut(i):
-            return LAST_CUT if i == last else CUT * steps[i][2] // HALF
-
         def interleave(copy, i, lo, hi):
-            g, c0, width = steps[i]
+            g, h = steps[i]
             copy(
-                out=grouped[i][:, lo:hi, :].rearrange("p (c i) t -> p c t i", i=4),
-                in_=raw[(g, c0)][:, :, lo:hi].rearrange("p t (c i) -> p c t i", i=4),
+                out=grouped[i][:, :, lo:hi, :].rearrange("p m q t -> p q t m"),
+                in_=raw[g][:].rearrange("p t (q m) -> p q t m", m=TILES)[:, lo:hi, :, h * HALF:(h + 1) * HALF],
             )
 
         def copy_scalar(i):
-            t = inter.tile([P, steps[i][2], PACK], BF16, align_bytes=64, name="grouped")
+            t = inter.tile([P, HALF, P, PACK], BF16, align_bytes=64, name="grouped")
             grouped[i] = t
-            interleave(nc.scalar.copy, i, 0, cut(i))
+            interleave(nc.scalar.copy, i, 0, CUT)
 
         def copy_vector(i):
-            interleave(nc.vector.tensor_copy, i, cut(i), steps[i][2])
+            interleave(nc.vector.tensor_copy, i, CUT, P)
 
         def quantise(i):
-            width = steps[i][2]
-            c = keep.tile([P, width], U32, align_bytes=64, name="codes_%d" % i)
-            s = keep.tile([P, width], U8, align_bytes=64, name="scales_%d" % i)
-            nc.vector.quantize_mx(out=c[:].bitcast(E4M3), scales=s[:], in_=grouped[i][:].rearrange("p w j -> p (w j)"))
+            c = keep.tile([P, HALF * P], U32, align_bytes=64, name="codes_%d" % i)
+            s = keep.tile([P, HALF * P], U8, align_bytes=64, name="scales_%d" % i)
+            nc.vector.quantize_mx(out=c[:].bitcast(E4M3), scales=s[:], in_=grouped[i][:].rearrange("p m q t -> p (m q t)"))
             codes[i], scales[i] = c, s
 
         def multiply(i):
-            g, c0, width = steps[i]
-            for m in range(width // P):
+            g, h = steps[i]
+            for m in range(HALF):
                 cols = slice(m * P, (m + 1) * P)
                 nc.tensor.matmul_mx(
-                    out=banks[c0 // P + m][:],
+                    out=banks[h * HALF + m][:],
                     lhsT=codes[i][:, cols].bitcast(E4M3),
                     lhsT_scale=scales[i][:, cols],
                     rhs=words[g][:].bitcast(E5M2),
@@ -143,6 +136,7 @@ def tile_boosted_leaf_refresh_e1_kernel(tc, member, grad_words, grad_scales, cur
 
         recip = {}
         diff = {}
+        result = {}
 
         def reciprocal(m):
             r = keep.tile([P, CLASSES], F32, name="recip_%d" % m)
@@ -159,36 +153,41 @@ def tile_boosted_leaf_refresh_e1_kernel(tc, member, grad_words, grad_scales, cur
             nc.vector.tensor_tensor(out=diff[m][:], in0=diff[m][:], in1=banks[m][:], op=SUB)
 
         def finish(m):
-            o = keep.tile([P, CLASSES], F32, name="result_%d" % m)
-            nc.vector.tensor_tensor(out=o[:], in0=diff[m][:], in1=recip[m][:], op=MUL)
-            nc.sync.dma_start(out=out[m * P:(m + 1) * P, :], in_=o[:])
+            if m % 2 == 0:
+                o = keep.tile([P, 2, CLASSES], F32, name="result_%d" % m)
+                result[m], result[m + 1] = o, o
+            nc.vector.tensor_tensor(out=result[m][:, m % 2, :], in0=diff[m][:], in1=recip[m][:], op=MUL)
+            if m >= TILES - 2:
+                nc.sync.dma_start(out=out_view[:, m, :], in_=result[m][:, m % 2, :])
+            elif m % 2 == 1:
+                nc.sync.dma_start(out=out_view[:, m - 1:m + 1, :], in_=result[m][:])
 
-        early = 8
-        half = TILES // 2
         for i in range(len(steps)):
             copy_scalar(i)
-            if early <= i < early + half:
-                reciprocal(i - early)
+            if i == 9:
+                reciprocal(0)
+                reciprocal(1)
             copy_vector(i)
             if i > 0:
                 quantise(i - 1)
                 multiply(i - 1)
-            if early <= i < early + half:
-                product(i - early)
-        for m in range(half, TILES):
+            if i == 9:
+                for m in range(HALF):
+                    product(m)
+        for m in range(2, TILES):
             reciprocal(m)
         quantise(last)
         multiply(last)
         subtract(0)
-        for m in range(1, half):
+        for m in range(1, HALF):
             subtract(m)
             finish(m - 1)
-        product(half)
-        finish(half - 1)
-        for m in range(half + 1, TILES):
+        product(HALF)
+        finish(HALF - 1)
+        for m in range(HALF + 1, TILES):
             product(m)
-        subtract(half)
-        for m in range(half + 1, TILES):
+        subtract(HALF)
+        for m in range(HALF + 1, TILES):
             subtract(m)
             finish(m - 1)
         finish(TILES - 1)

@@ -23,7 +23,9 @@ PACK = 4
 GROUPS = K // (P * PACK)
 TILES = LEAVES // P
 HALF = TILES // 2
-CUT = 66
+CUT = 68
+PAUSE = 4
+LATE = 3
 
 
 def tile_boosted_leaf_refresh_e1_kernel(tc, member, grad_words, grad_scales, curv, old, out):
@@ -46,11 +48,10 @@ def tile_boosted_leaf_refresh_e1_kernel(tc, member, grad_words, grad_scales, cur
         g_scales = keep.tile([P, GROUPS, CLASSES], U8, align_bytes=64, name="g_scales")
         nc.vector.memset(g_scales[:].rearrange("p g n -> p (g n)").bitcast(I32), 0)
 
-        def load_member(g, lo, hi):
-            if g not in raw:
-                t = keep.tile([P, PACK, LEAVES], BF16, align_bytes=64, name="raw_%d" % g)
-                raw[g] = t
-            nc.sync.dma_start(out=raw[g][:, :, lo:hi], in_=a_view[g, :, :, lo:hi])
+        def load_member(g):
+            t = keep.tile([P, PACK, LEAVES], BF16, align_bytes=64, name="raw_%d" % g)
+            nc.sync.dma_start(out=t[:], in_=a_view[g])
+            raw[g] = t
 
         def load_words(g):
             t = keep.tile([P, CLASSES], U32, align_bytes=64, name="words_%d" % g)
@@ -74,18 +75,18 @@ def tile_boosted_leaf_refresh_e1_kernel(tc, member, grad_words, grad_scales, cur
                     in_=grad_scales[:, 4 * q:4 * q + 4, :].rearrange("g r n -> r g n").bitcast(I32),
                 )
 
-        load_member(0, 0, TILES * CUT)
-        load_member(0, TILES * CUT, LEAVES)
-        load_member(1, 0, LEAVES)
+        load_member(0)
+        load_member(1)
         load_scales()
         load_words(0)
         for g in range(2, GROUPS):
-            if g == 5:
+            if g == PAUSE:
                 load_old_curv(0)
-            if g == GROUPS - 1:
+            load_member(g)
+            if g - 1 < GROUPS - LATE:
                 load_words(g - 1)
-            load_member(g, 0, LEAVES)
-            load_words(g if g == GROUPS - 1 else g - 1)
+        for g in range(GROUPS - LATE, GROUPS):
+            load_words(g)
         load_old_curv(1)
 
         steps = [(g, h) for g in range(GROUPS) for h in range(2)]
@@ -162,22 +163,27 @@ def tile_boosted_leaf_refresh_e1_kernel(tc, member, grad_words, grad_scales, cur
             elif m % 2 == 1:
                 nc.sync.dma_start(out=out_view[:, m - 1:m + 1, :], in_=result[m][:])
 
+        pause = 2 * PAUSE - 1
+        early = 3
         for i in range(len(steps)):
             copy_scalar(i)
-            if i == 9:
-                reciprocal(0)
-                reciprocal(1)
+            if i == pause:
+                for m in range(early):
+                    reciprocal(m)
             copy_vector(i)
             if i > 0:
                 quantise(i - 1)
-                multiply(i - 1)
-            if i == 9:
+                g, h = steps[i - 1]
+                if h == 0 or g < GROUPS - LATE:
+                    multiply(i - 1)
+            if i == pause:
                 for m in range(HALF):
                     product(m)
-        for m in range(2, TILES):
+        for m in range(early, TILES):
             reciprocal(m)
         quantise(last)
-        multiply(last)
+        for g in range(GROUPS - LATE, GROUPS):
+            multiply(2 * g + 1)
         subtract(0)
         for m in range(1, HALF):
             subtract(m)
@@ -190,4 +196,8 @@ def tile_boosted_leaf_refresh_e1_kernel(tc, member, grad_words, grad_scales, cur
         for m in range(HALF + 1, TILES):
             subtract(m)
             finish(m - 1)
-        finish(TILES - 1)
+        m = TILES - 1
+        for c in range(2):
+            cols = slice(c * CLASSES // 2, (c + 1) * CLASSES // 2)
+            nc.vector.tensor_tensor(out=result[m][:, 1, cols], in0=diff[m][:, cols], in1=recip[m][:, cols], op=MUL)
+            nc.sync.dma_start(out=out_view[:, m, cols], in_=result[m][:, 1, cols])

@@ -23,9 +23,9 @@ PACK = 4
 GROUPS = K // (P * PACK)
 TILES = LEAVES // P
 HALF = TILES // 2
-CUT = 68
+CUT = 64
 PAUSE = 4
-LATE = 3
+LATE = 2
 
 
 def tile_boosted_leaf_refresh_e1_kernel(tc, member, grad_words, grad_scales, curv, old, out):
@@ -153,18 +153,21 @@ def tile_boosted_leaf_refresh_e1_kernel(tc, member, grad_words, grad_scales, cur
         def subtract(m):
             nc.vector.tensor_tensor(out=diff[m][:], in0=diff[m][:], in1=banks[m][:], op=SUB)
 
-        def finish(m):
+        def finish(m, engine=nc.vector, parts=1):
             if m % 2 == 0:
                 o = keep.tile([P, 2, CLASSES], F32, name="result_%d" % m)
                 result[m], result[m + 1] = o, o
-            nc.vector.tensor_tensor(out=result[m][:, m % 2, :], in0=diff[m][:], in1=recip[m][:], op=MUL)
-            if m >= TILES - 2:
-                nc.sync.dma_start(out=out_view[:, m, :], in_=result[m][:, m % 2, :])
-            elif m % 2 == 1:
+            width = CLASSES // parts
+            for c in range(parts):
+                cols = slice(c * width, (c + 1) * width)
+                engine.tensor_tensor(out=result[m][:, m % 2, cols], in0=diff[m][:, cols], in1=recip[m][:, cols], op=MUL)
+                if m >= TILES - 2:
+                    nc.sync.dma_start(out=out_view[:, m, cols], in_=result[m][:, m % 2, cols])
+            if m < TILES - 2 and m % 2 == 1:
                 nc.sync.dma_start(out=out_view[:, m - 1:m + 1, :], in_=result[m][:])
 
         pause = 2 * PAUSE - 1
-        early = 3
+        early = 2
         for i in range(len(steps)):
             copy_scalar(i)
             if i == pause:
@@ -184,20 +187,14 @@ def tile_boosted_leaf_refresh_e1_kernel(tc, member, grad_words, grad_scales, cur
         quantise(last)
         for g in range(GROUPS - LATE, GROUPS):
             multiply(2 * g + 1)
-        subtract(0)
-        for m in range(1, HALF):
-            subtract(m)
-            finish(m - 1)
-        product(HALF)
-        finish(HALF - 1)
-        for m in range(HALF + 1, TILES):
-            product(m)
-        subtract(HALF)
-        for m in range(HALF + 1, TILES):
-            subtract(m)
-            finish(m - 1)
-        m = TILES - 1
-        for c in range(2):
-            cols = slice(c * CLASSES // 2, (c + 1) * CLASSES // 2)
-            nc.vector.tensor_tensor(out=result[m][:, 1, cols], in0=diff[m][:, cols], in1=recip[m][:, cols], op=MUL)
-            nc.sync.dma_start(out=out_view[:, m, cols], in_=result[m][:, 1, cols])
+        for h in range(2):
+            tiles = range(h * HALF, (h + 1) * HALF)
+            if h == 1:
+                for m in tiles:
+                    product(m)
+            for m in tiles:
+                subtract(m)
+                if m == tiles[0]:
+                    finish(m, engine=nc.gpsimd)
+            for m in tiles[1:]:
+                finish(m, parts=2 if m == TILES - 1 else 1)

from contextlib import ExitStack

import concourse.mybir as mybir

K, LEAVES, CLASSES = 4096, 1024, 512
FLOPS = 2 * K * LEAVES * CLASSES

F32 = mybir.dt.float32
BF16 = mybir.dt.bfloat16
U32 = mybir.dt.uint32
I32 = mybir.dt.int32
U8 = mybir.dt.uint8
E4M3 = mybir.dt.float8_e4m3fn_x4
E5M2 = mybir.dt.float8_e5m2_x4
ADD = mybir.AluOpType.add
SUB = mybir.AluOpType.subtract
MUL = mybir.AluOpType.mult
RSQRT = mybir.ActivationFunctionType.Abs_reciprocal_sqrt
SQUARE = mybir.ActivationFunctionType.Square

P = 128
PACK = 4
GROUPS = K // (P * PACK)
TILES = LEAVES // P
HALF = TILES // 2
CUT = 64
PAUSE = 4
LATE = 2


def tile_boosted_leaf_refresh_e1_kernel(tc, member, grad_words, grad_scales, curv, old, out):
    nc = tc.nc
    with ExitStack() as ctx:
        keep = ctx.enter_context(tc.tile_pool(name="keep", bufs=1))
        inter = ctx.enter_context(tc.tile_pool(name="inter", bufs=4))
        psum = ctx.enter_context(tc.psum_pool(name="psum", bufs=1))
        ctx.enter_context(tc.manual_schedule())

        a_view = member.rearrange("(g p j) w -> g p j w", p=P, j=PACK)
        out_view = out.rearrange("(p m) n -> p m n", m=TILES)
        raw = {}
        words = {}

        one = keep.tile([P, 1], F32, name="one")
        nc.vector.memset(one[:], 1.0)
        warm = keep.tile([P, 1], F32, name="warm")
        nc.scalar.activation(out=warm[:], in_=one[:], func=RSQRT, bias=one[:], scale=1.0)
        g_scales = keep.tile([P, GROUPS, CLASSES], U8, align_bytes=64, name="g_scales")
        nc.vector.memset(g_scales[:].rearrange("p g n -> p (g n)").bitcast(I32), 0)

        def load_member(g):
            t = keep.tile([P, PACK, LEAVES], BF16, align_bytes=64, name="raw_%d" % g)
            nc.sync.dma_start(out=t[:], in_=a_view[g])
            raw[g] = t

        def load_words(g):
            t = keep.tile([P, CLASSES], U32, align_bytes=64, name="words_%d" % g)
            nc.sync.dma_start(out=t[:].bitcast(I32), in_=grad_words[g].rearrange("p n t -> p (n t)").bitcast(I32))
            words[g] = t

        curv_t = {}
        old_t = {}

        def load_old_curv(h):
            for src, dst, nm in ((curv, curv_t, "curv"), (old, old_t, "old")):
                t = keep.tile([P, HALF, CLASSES], BF16, align_bytes=64, name="%s_%d" % (nm, h))
                nc.sync.dma_start(out=t[:], in_=src.rearrange("(p m) n -> p m n", m=TILES)[:, h * HALF:(h + 1) * HALF, :])
                for m in range(HALF):
                    dst[h * HALF + m] = t[:, m, :]

        def load_scales():
            for q in range(4):
                nc.sync.dma_start(
                    out=g_scales[32 * q:32 * q + 4, :, :].bitcast(I32),
                    in_=grad_scales[:, 4 * q:4 * q + 4, :].rearrange("g r n -> r g n").bitcast(I32),
                )

        load_member(0)
        load_member(1)
        load_scales()
        load_words(0)
        for g in range(2, GROUPS):
            if g == PAUSE:
                load_old_curv(0)
            load_member(g)
            if g - 1 < GROUPS - LATE:
                load_words(g - 1)
        for g in range(GROUPS - LATE, GROUPS):
            load_words(g)
        load_old_curv(1)

        steps = [(g, h) for g in range(GROUPS) for h in range(2)]
        last = len(steps) - 1

        banks = []
        for m in range(TILES):
            bank = psum.tile([P, CLASSES], F32, name="bank_%d" % m)
            banks.append(bank)
        grouped = {}
        codes = {}
        scales = {}

        def interleave(copy, i, lo, hi):
            g, h = steps[i]
            copy(
                out=grouped[i][:, :, lo:hi, :].rearrange("p m q t -> p q t m"),
                in_=raw[g][:].rearrange("p t (q m) -> p q t m", m=TILES)[:, lo:hi, :, h * HALF:(h + 1) * HALF],
            )

        def copy_scalar(i):
            t = inter.tile([P, HALF, P, PACK], BF16, align_bytes=64, name="grouped")
            grouped[i] = t
            interleave(nc.scalar.copy, i, 0, CUT)

        def copy_vector(i):
            interleave(nc.vector.tensor_copy, i, CUT, P)

        def quantise(i):
            c = keep.tile([P, HALF * P], U32, align_bytes=64, name="codes_%d" % i)
            s = keep.tile([P, HALF * P], U8, align_bytes=64, name="scales_%d" % i)
            nc.vector.quantize_mx(out=c[:].bitcast(E4M3), scales=s[:], in_=grouped[i][:].rearrange("p m q t -> p (m q t)"))
            codes[i], scales[i] = c, s

        def multiply(i):
            g, h = steps[i]
            for m in range(HALF):
                cols = slice(m * P, (m + 1) * P)
                nc.tensor.matmul_mx(
                    out=banks[h * HALF + m][:],
                    lhsT=codes[i][:, cols].bitcast(E4M3),
                    lhsT_scale=scales[i][:, cols],
                    rhs=words[g][:].bitcast(E5M2),
                    rhs_scale=g_scales[:, g, :],
                    start=(g == 0),
                    stop=(g == GROUPS - 1),
                )

        recip = {}
        diff = {}
        result = {}

        def reciprocal(m):
            r = keep.tile([P, CLASSES], F32, name="recip_%d" % m)
            nc.scalar.activation(out=r[:], in_=curv_t[m], func=RSQRT, bias=one[:], scale=1.0)
            nc.scalar.activation(out=r[:], in_=r[:], func=SQUARE)
            recip[m] = r

        def product(m):
            d = keep.tile([P, CLASSES], F32, name="diff_%d" % m)
            nc.vector.tensor_tensor(out=d[:], in0=curv_t[m], in1=old_t[m], op=MUL)
            diff[m] = d

        def subtract(m):
            nc.vector.tensor_tensor(out=diff[m][:], in0=diff[m][:], in1=banks[m][:], op=SUB)

        def finish(m, engine=nc.vector, parts=1):
            if m % 2 == 0:
                o = keep.tile([P, 2, CLASSES], F32, name="result_%d" % m)
                result[m], result[m + 1] = o, o
            width = CLASSES // parts
            for c in range(parts):
                cols = slice(c * width, (c + 1) * width)
                engine.tensor_tensor(out=result[m][:, m % 2, cols], in0=diff[m][:, cols], in1=recip[m][:, cols], op=MUL)
                if m >= TILES - 2:
                    nc.sync.dma_start(out=out_view[:, m, cols], in_=result[m][:, m % 2, cols])
            if m < TILES - 2 and m % 2 == 1:
                nc.sync.dma_start(out=out_view[:, m - 1:m + 1, :], in_=result[m][:])

        pause = 2 * PAUSE - 1
        early = 2
        for i in range(len(steps)):
            copy_scalar(i)
            if i == pause:
                for m in range(early):
                    reciprocal(m)
            copy_vector(i)
            if i > 0:
                quantise(i - 1)
                g, h = steps[i - 1]
                if h == 0 or g < GROUPS - LATE:
                    multiply(i - 1)
            if i == pause:
                for m in range(HALF):
                    product(m)
        for m in range(early, TILES):
            reciprocal(m)
        quantise(last)
        for g in range(GROUPS - LATE, GROUPS):
            multiply(2 * g + 1)
        for h in range(2):
            tiles = range(h * HALF, (h + 1) * HALF)
            if h == 1:
                for m in tiles:
                    product(m)
            for m in tiles:
                subtract(m)
                if m == tiles[0]:
                    finish(m, engine=nc.gpsimd)
            for m in tiles[1:]:
                finish(m, parts=2 if m == TILES - 1 else 1)
